import numpy as np
import ml_dtypes


def mxq(x, axis, fmt="e4m3"):
    dtype, down = {"e4m3": (ml_dtypes.float8_e4m3fn, 7), "e5m2": (ml_dtypes.float8_e5m2, 14)}[fmt]
    v = np.moveaxis(np.asarray(x, np.float32).astype(ml_dtypes.bfloat16).astype(np.float64), axis, -1)
    blocks = v.reshape(v.shape[:-1] + (-1, 32))
    amax = np.abs(blocks).max(-1, keepdims=True)
    byte = np.maximum(np.where(amax > 0, np.frexp(amax)[1] - 1 + 127, 0) - down, 1)
    scale = np.exp2(byte - 127.0)
    codes = (blocks / scale).astype(np.float32).astype(dtype).astype(np.float64)
    return np.moveaxis((codes * scale).reshape(v.shape), -1, axis)


WIDE = False


def mx_kscale(k):
    if not WIDE:
        return np.ones(k)
    levels = np.array([10, -10, 5, -5, 0])
    if k % 512:
        return np.exp2(np.random.permutation(np.resize(levels, k // 32))).repeat(32)
    a = np.empty((k // 512, 16))
    for p in range(k // 512):
        a[p, :8] = np.random.permutation(np.resize(levels, 8))
        for g in range(8):
            far = levels[np.abs(levels - a[p, g]) >= 10]
            a[p, g + 8] = far[np.random.randint(len(far))]
    return np.exp2(a.ravel()).repeat(32)


def f64(x):
    return np.asarray(x).astype(np.float64)


def striped(idx):
    return np.tile(idx.reshape(-1, 16).T, (8, 1)).astype(np.uint16)


def unstriped(offs):
    return offs[:16].T.reshape(-1).astype(np.int64)


def striped8(idx):
    return np.concatenate([x.reshape(-1, 16).T for x in idx]).astype(np.uint16)


def runs(offs, k):
    lists = np.stack([offs[16 * r : 16 * r + 16].T.reshape(-1) for r in range(8)]).astype(np.int64)
    return lists[np.arange(k) % 512 // 64]


def pack_weight(w):
    k, n = w.shape
    w = f64(np.asarray(w, np.float32).astype(ml_dtypes.bfloat16)).reshape(k // 32, 32, n)
    amax = np.abs(w).max(1)
    byte = np.clip(np.where(amax > 0, np.frexp(amax)[1] - 1 + 127 - 7, 1), 1, 254)
    scaled = (w * np.exp2(127.0 - byte)[:, None, :]).reshape(k, n).astype(np.float32)
    words = np.ascontiguousarray(scaled.reshape(k // 512, 128, 4, n).transpose(0, 1, 3, 2)).astype(ml_dtypes.float8_e4m3fn).view(np.uint8)
    return words, np.ascontiguousarray(byte.astype(np.uint8).reshape(k // 512, 16, n))


def unpack_weight(words, scales):
    g, p, n, _ = words.shape
    vals = np.ascontiguousarray(words).view(ml_dtypes.float8_e4m3fn).astype(np.float64) * np.repeat(np.exp2(scales.astype(np.float64) - 127.0), 8, axis=1)[..., None]
    return vals.transpose(0, 1, 3, 2).reshape(g * 512, n)


def sigmoid(v):
    return 1.0 / (1.0 + np.exp(-np.maximum(v, -700.0)))


K, T, S, N, H, U = 512, 2048, 512, 512, 512, 1024


def setup_inputs():
    n = np.random.standard_normal
    s = mx_kscale(K)[:, None]
    u = mx_kscale(H)
    packed_xT = pack_weight(n((K, T)) * s)
    return {
        "x_words": packed_xT[0],
        "x_scales": packed_xT[1],
        "w1": (n((K, H)) / np.sqrt(K) / s).astype(np.float32),
        "w2": (n((K, H)) / np.sqrt(K) / s).astype(np.float32),
        "gn": (np.random.uniform(0.5, 1.5, (H, 1)) * u[:, None]).astype(np.float32),
        "w3": (n((H, N)) / np.sqrt(H) / u[:, None]).astype(np.float32),
        "mem": n((N, U)).astype(np.float32),
        "offs": striped(np.random.permutation(T)[:S]),
        "hz": striped8(np.random.randint(0, T, (8, S))),
        "n1": striped8(np.stack([np.random.permutation(S) for _ in range(8)])),
        "n2": striped8(np.stack([np.random.permutation(S) for _ in range(8)])),
        "n3": striped(np.random.permutation(U)[:S]),
    }


def reference(x_words, x_scales, w1, w2, gn, w3, mem, offs, hz, n1, n2, n3):
    old = f64(mem)[:, unstriped(n3)]
    xq = unpack_weight(x_words, x_scales)[:, unstriped(offs)]
    y = mxq(f64(w1), 0, "e4m3").T @ xq
    x_hz = unpack_weight(x_words, x_scales)[np.arange(K)[:, None], runs(hz, K)]
    d = mxq(f64(w2), 0, "e4m3").T @ x_hz
    z = f64(gn) * ((y - (y[np.arange(H)[:, None], runs(n1, H)])) / (np.abs(d) + np.abs(d[np.arange(H)[:, None], runs(n2, H)]) + 0.5))
    h = mxq(f64(w3), 0, "e4m3").T @ mxq(z, 0, "e4m3")
    nw = old + sigmoid(h) * (h - old)
    out = f64(mem).copy()
    out[:, unstriped(n3)] = nw
    return out

@@ -1,0 +1,300 @@
+from contextlib import ExitStack
+
+import concourse.mybir as mybir
+
+K, T, S, H, N, U = 512, 2048, 512, 512, 512, 1024
+FLOPS = 2 * S * (2 * K * H + H * N)
+
+F32 = mybir.dt.float32
+BF16 = mybir.dt.bfloat16
+I32 = mybir.dt.int32
+U32 = mybir.dt.uint32
+U16 = mybir.dt.uint16
+U8 = mybir.dt.uint8
+FP8X4 = mybir.dt.float8_e4m3fn_x4
+ALU = mybir.AluOpType
+ACT = mybir.ActivationFunctionType
+
+P = 128
+PACK = 4
+HALF = S // 2
+LIST_COLS = S // 16
+
+
+def tile_picked_twhnormbpaget_none_p_kernel(
+    tc, x_words, x_scales, w1, w2, gn, w3, mem, offs, hz, n1, n2, n3, out
+):
+    nc = tc.nc
+    halves = [slice(0, HALF), slice(HALF, S)]
+    list_halves = [slice(0, LIST_COLS // 2), slice(LIST_COLS // 2, LIST_COLS)]
+
+    with ExitStack() as ctx:
+        sb = ctx.enter_context(tc.tile_pool(name="sb", bufs=1))
+        psum = ctx.enter_context(tc.psum_pool(name="psum", bufs=1))
+
+        def tile(name, shape, dtype):
+            return sb.tile(shape, dtype, name=name, align_bytes=64)
+
+        def load_list(name, src):
+            dst = tile(name, [P, LIST_COLS], U16)
+            nc.sync.dma_start(dst[:], src)
+            return dst
+
+        def load_weight(name, src):
+            dst = tile(name, [P, PACK, 512], F32)
+            nc.sync.dma_start(dst[:], src.rearrange("(p j) c -> p j c", j=PACK))
+            return dst
+
+        xs = tile("xs", [P, T], U8)
+        rows = x_scales[0].bitcast(I32)
+        for q in range(4):
+            nc.sync.dma_start(
+                xs[32 * q : 32 * (q + 1), :].bitcast(I32),
+                rows[4 * q : 4 * (q + 1), :].unsqueeze(0).broadcast_to([8, 4, T // 4]),
+            )
+        hz_t = load_list("hz_t", hz)
+        offs_t = load_list("offs_t", offs)
+        xw = tile("xw", [P, T], U32)
+        nc.sync.dma_start(xw[:].bitcast(I32), x_words[0].rearrange("p n t -> p (n t)").bitcast(I32))
+        w1_raw = load_weight("w1_raw", w1)
+        w2_raw = load_weight("w2_raw", w2)
+        n1_t = load_list("n1_t", n1)
+        n2_t = load_list("n2_t", n2)
+        gn_t = tile("gn_t", [P, PACK], F32)
+        nc.sync.dma_start(gn_t[:], gn.rearrange("(p t) o -> p (t o)", t=PACK))
+        w3_raw = load_weight("w3_raw", w3)
+        n3_t = load_list("n3_t", n3)
+        page = []
+        for u in range(4):
+            page.append(tile("page%d" % u, [P, U], F32))
+            nc.sync.dma_start(page[u][:], mem[u * P : (u + 1) * P, :])
+        half_c = tile("half_c", [P, 1], F32)
+        nc.gpsimd.memset(half_c[:], 0.5)
+
+        hz_bytes = tile("hz_bytes", [P, S], U8)
+        nc.vector.tensor_copy(hz_bytes[:], xs[:].indirect(hz_t[:]))
+        hz_plane = tile("hz_plane", [P, S], U8)
+        nc.vector.tensor_copy(hz_plane[:].bitcast(I32), hz_bytes[:].bitcast(I32))
+        for r in range(2, 4):
+            nc.scalar.dma_start(hz_plane[r:P:32, :].bitcast(I32), hz_bytes[16 + r : P : 32, :].bitcast(I32))
+        tok_plane = tile("tok_plane", [P, S], U8)
+        nc.vector.tensor_copy(tok_plane[:], xs[:].indirect(offs_t[:]))
+        tok_words = tile("tok_words", [P, S], U32)
+        nc.vector.tensor_copy(tok_words[:], xw[:].indirect(offs_t[:]))
+        hz_words = tile("hz_words", [P, S], U32)
+        nc.vector.tensor_copy(hz_words[:], xw[:].indirect(hz_t[:]))
+
+        def dealt_views(grouped, raw, ts):
+            dst = grouped[:].rearrange("p (t m j) -> p m j t", t=PACK, j=PACK)[:, :, :, ts]
+            src = raw[:].rearrange("p j (m t) -> p m j t", t=PACK)[:, :, :, ts]
+            return dst, src
+
+        def quantize(codes, plane, grouped, cols):
+            nc.vector.quantize_mx(
+                out=codes[:, cols].bitcast(FP8X4),
+                scales=plane[:, cols],
+                in_=grouped[:, PACK * cols.start : PACK * cols.stop],
+            )
+
+        def product(acc, w_codes, w_plane, t, words, plane):
+            cols = slice(t * P, (t + 1) * P)
+            nc.tensor.matmul_mx(
+                out=acc,
+                lhsT=w_codes[:, cols].bitcast(FP8X4),
+                lhsT_scale=w_plane[:, cols],
+                rhs=words.bitcast(FP8X4),
+                rhs_scale=plane,
+                start=True,
+                stop=True,
+            )
+
+        w1_bf = tile("w1_bf", [P, PACK * H], BF16)
+        w1_codes = tile("w1_codes", [P, H], U32)
+        w1_plane = tile("w1_plane", [P, H], U8)
+        dst, src = dealt_views(w1_bf, w1_raw, slice(0, 2))
+        nc.scalar.activation(out=dst, in_=src, func=ACT.Copy)
+        dst, src = dealt_views(w1_bf, w1_raw, slice(2, 4))
+        nc.vector.tensor_copy(dst, src)
+        quantize(w1_codes, w1_plane, w1_bf, halves[1])
+        quantize(w1_codes, w1_plane, w1_bf, halves[0])
+        order = [2, 3, 0, 1]
+        y_ps, y_sb = {}, {}
+        for t in order:
+            y_ps[t] = psum.tile([P, S], F32, name="bank_y%d" % t)
+            product(y_ps[t][:], w1_codes, w1_plane, t, tok_words[:], tok_plane[:])
+        for t in order:
+            y_sb[t] = tile("y_sb%d" % t, [P, S], F32)
+            nc.scalar.copy(y_sb[t][:], y_ps[t][:])
+
+        w2_bf = tile("w2_bf", [P, PACK * H], BF16)
+        w2_codes = tile("w2_codes", [P, H], U32)
+        w2_plane = tile("w2_plane", [P, H], U8)
+        dst, src = dealt_views(w2_bf, w2_raw, slice(0, 4))
+        nc.vector.tensor_copy(dst, src)
+        quantize(w2_codes, w2_plane, w2_bf, slice(0, H))
+        size = {}
+        for t in order:
+            d_ps = psum.tile([P, S], F32, name="bank_d%d" % t)
+            product(d_ps[:], w2_codes, w2_plane, t, hz_words[:], hz_plane[:])
+            size[t] = tile("size%d" % t, [P, S], F32)
+            nc.scalar.activation(out=size[t][:], in_=d_ps[:], func=ACT.Abs)
+
+        y_far = tile("y_far", [P, PACK, S], F32)
+        size_far = tile("size_far", [P, PACK, S], F32)
+        num = tile("num", [P, PACK, S], F32)
+        den = tile("den", [P, PACK, S], F32)
+        root = tile("root", [P, PACK, S], F32)
+        part = tile("part", [P, PACK, S], F32)
+        w3_bf = tile("w3_bf", [P, PACK * N], BF16)
+        w3_codes = tile("w3_codes", [P, N], U32)
+        w3_plane = tile("w3_plane", [P, N], U8)
+        z_bf = tile("z_bf", [P, PACK * S], BF16)
+        z_codes = tile("z_codes", [P, S], U32)
+        z_plane = tile("z_plane", [P, S], U8)
+        quads = [slice(0, HALF // 4), slice(HALF // 4, S // 4)]
+        old, gate, gap, step, new, h_ps = {}, {}, {}, {}, {}, {}
+        for u in range(4):
+            old[u] = tile("old%d" % u, [P, S], F32)
+            gate[u] = tile("gate%d" % u, [P, S], F32)
+            gap[u] = tile("gap%d" % u, [P, S], F32)
+            step[u] = tile("step%d" % u, [P, S], F32)
+        for u in range(3):
+            new[u] = tile("new%d" % u, [P, S], F32)
+
+        def fetch(on_scalar, dst, window):
+            if on_scalar:
+                nc.scalar.activation(out=dst, in_=window, func=ACT.Copy)
+            else:
+                nc.vector.tensor_copy(dst, window)
+
+        def fetch_y(on_scalar, t, a):
+            fetch(on_scalar, y_far[:, t, halves[a]], y_sb[t][:].indirect(n1_t[:, list_halves[a]]))
+
+        def fetch_size(t, a):
+            fetch(True, size_far[:, t, halves[a]], size[t][:].indirect(n2_t[:, list_halves[a]]))
+
+        def make_num(t, a):
+            nc.vector.tensor_tensor(num[:, t, halves[a]], y_ps[t][:, halves[a]], y_far[:, t, halves[a]], ALU.subtract)
+
+        def make_den(t, a):
+            nc.vector.tensor_tensor(den[:, t, halves[a]], size[t][:, halves[a]], size_far[:, t, halves[a]], ALU.add)
+
+        def make_root(a):
+            nc.scalar.activation(
+                out=root[:, :, halves[a]], in_=den[:, :, halves[a]], func=ACT.Abs_reciprocal_sqrt, bias=half_c[:], scale=1.0
+            )
+
+        def make_part(t, a):
+            nc.vector.scalar_tensor_tensor(
+                part[:, t, halves[a]], num[:, t, halves[a]], gn_t[:, t : t + 1], root[:, t, halves[a]], ALU.mult, ALU.mult
+            )
+
+        def make_z(a):
+            nc.vector.tensor_tensor(
+                z_bf[:].rearrange("p (c i t) -> p c t i", i=4, t=PACK)[:, quads[a]],
+                part[:].rearrange("p t (c i) -> p c t i", i=4)[:, quads[a]],
+                root[:].rearrange("p t (c i) -> p c t i", i=4)[:, quads[a]],
+                ALU.mult,
+            )
+
+        def make_h(a):
+            quantize(z_codes, z_plane, z_bf, halves[a])
+            for u in range(4):
+                bank = psum.tile([P, S], F32, name=("bank_d%d", "bank_y%d")[a] % u)
+                h_ps[u, a] = bank[:, 0:HALF]
+                product(h_ps[u, a], w3_codes, w3_plane, u, z_codes[:, halves[a]], z_plane[:, halves[a]])
+
+        def fetch_old(on_scalar, u):
+            fetch(on_scalar, old[u][:], page[u][:].indirect(n3_t[:]))
+
+        def make_gate(u, a):
+            nc.scalar.activation(out=gate[u][:, halves[a]], in_=h_ps[u, a], func=ACT.Sigmoid)
+
+        def make_gap(u, a):
+            nc.vector.tensor_tensor(gap[u][:, halves[a]], h_ps[u, a], old[u][:, halves[a]], ALU.subtract)
+
+        def make_step(u):
+            nc.vector.tensor_tensor(step[u][:], gap[u][:], gate[u][:], ALU.mult)
+
+        def make_new(u, cols):
+            nc.vector.tensor_tensor(new[u][:, cols], step[u][:, cols], old[u][:, cols], ALU.add)
+
+        def put_scalar(u, a):
+            nc.scalar.activation(
+                out=page[u][:].indirect(n3_t[:, list_halves[a]]), in_=new[u][:, halves[a]], func=ACT.Copy
+            )
+
+        def store(u):
+            nc.sync.dma_start(out[u * P : (u + 1) * P, :], page[u][:])
+
+        for t in order:
+            fetch_y(False, t, 0)
+        for a in range(2):
+            for t in order:
+                fetch_size(t, a)
+        for t in order:
+            make_num(t, 0)
+        nc.vector.tensor_copy(
+            w3_bf[:].rearrange("p (c i j) -> p c j i", i=4, j=PACK),
+            w3_raw[:].rearrange("p j (c i) -> p c j i", i=4),
+        )
+        for t in order:
+            make_den(t, 0)
+        quantize(w3_codes, w3_plane, w3_bf, slice(0, N))
+        for t in order[:2]:
+            fetch_y(True, t, 1)
+        for t in order:
+            make_den(t, 1)
+        for t in order[2:]:
+            fetch_y(False, t, 1)
+        make_root(0)
+        make_root(1)
+        for t in order:
+            make_num(t, 1)
+        for t in order:
+            make_part(t, 0)
+        fetch_old(True, 0)
+        make_part(order[0], 1)
+        make_z(0)
+        make_part(order[1], 1)
+        make_h(0)
+        for t in order[2:]:
+            make_part(t, 1)
+        make_gate(0, 0)
+        fetch_old(True, 1)
+        make_gap(0, 0)
+        make_z(1)
+        make_gap(1, 0)
+        make_h(1)
+        for u in range(1, 4):
+            make_gate(u, 0)
+        for u in range(2):
+            make_gate(u, 1)
+        fetch_old(False, 2)
+        make_gap(0, 1)
+        make_gap(1, 1)
+        make_step(0)
+        fetch_old(True, 3)
+        for u in range(2, 4):
+            make_gate(u, 1)
+        make_step(1)
+        make_new(0, slice(0, S))
+        make_gap(2, 0)
+        make_new(1, slice(0, S))
+        make_gap(2, 1)
+        for u in range(2):
+            put_scalar(u, 0)
+            put_scalar(u, 1)
+            store(u)
+        make_gap(3, 0)
+        make_step(2)
+        make_gap(3, 1)
+        make_new(2, halves[0])
+        make_step(3)
+        nc.vector.tensor_tensor(
+            page[2][:].indirect(n3_t[:, list_halves[1]]), step[2][:, halves[1]], old[2][:, halves[1]], ALU.add
+        )
+        put_scalar(2, 0)
+        nc.vector.tensor_tensor(page[3][:].indirect(n3_t[:]), step[3][:], old[3][:], ALU.add)
+        store(3)
+        store(2)

@@ -19,30 +19,31 @@ P = 128
 PACK = 4
 HALF = S // 2
 LIST_COLS = S // 16
+SCALAR_SHARE = 320
 
 
 def tile_picked_twhnormbpaget_none_p_kernel(
     tc, x_words, x_scales, w1, w2, gn, w3, mem, offs, hz, n1, n2, n3, out
 ):
     nc = tc.nc
+    whole = slice(0, S)
     halves = [slice(0, HALF), slice(HALF, S)]
-    list_halves = [slice(0, LIST_COLS // 2), slice(LIST_COLS // 2, LIST_COLS)]
 
     with ExitStack() as ctx:
         sb = ctx.enter_context(tc.tile_pool(name="sb", bufs=1))
         psum = ctx.enter_context(tc.psum_pool(name="psum", bufs=1))
 
-        def tile(name, shape, dtype):
-            return sb.tile(shape, dtype, name=name, align_bytes=64)
+        def tile(name, shape, dtype, tag=None):
+            return sb.tile(shape, dtype, name=name, tag=tag or name, align_bytes=64)
 
         def load_list(name, src):
             dst = tile(name, [P, LIST_COLS], U16)
             nc.sync.dma_start(dst[:], src)
             return dst
 
-        def load_weight(name, src):
-            dst = tile(name, [P, PACK, 512], F32)
-            nc.sync.dma_start(dst[:], src.rearrange("(p j) c -> p j c", j=PACK))
+        def load_weight(name, src, cols):
+            dst = tile(name, [P, PACK, cols.stop - cols.start], F32)
+            nc.sync.dma_start(dst[:], src.rearrange("(p j) c -> p j c", j=PACK)[:, :, cols])
             return dst
 
         xs = tile("xs", [P, T], U8)
@@ -56,20 +57,28 @@ def tile_picked_twhnormbpaget_none_p_kernel(
         offs_t = load_list("offs_t", offs)
         xw = tile("xw", [P, T], U32)
         nc.sync.dma_start(xw[:].bitcast(I32), x_words[0].rearrange("p n t -> p (n t)").bitcast(I32))
-        w1_raw = load_weight("w1_raw", w1)
-        w2_raw = load_weight("w2_raw", w2)
-        n1_t = load_list("n1_t", n1)
+        w2_raw = [load_weight("w2_raw%d" % a, w2, halves[a]) for a in range(2)]
+        w1_raw = load_weight("w1_raw", w1, whole)
         n2_t = load_list("n2_t", n2)
+        n1_t = load_list("n1_t", n1)
         gn_t = tile("gn_t", [P, PACK], F32)
         nc.sync.dma_start(gn_t[:], gn.rearrange("(p t) o -> p (t o)", t=PACK))
-        w3_raw = load_weight("w3_raw", w3)
         n3_t = load_list("n3_t", n3)
+        w3_raw = load_weight("w3_raw", w3, whole)
         page = []
         for u in range(4):
             page.append(tile("page%d" % u, [P, U], F32))
             nc.sync.dma_start(page[u][:], mem[u * P : (u + 1) * P, :])
         half_c = tile("half_c", [P, 1], F32)
         nc.gpsimd.memset(half_c[:], 0.5)
+        y_sb, size = [], []
+        for t in range(PACK):
+            y_sb.append(tile("y_sb%d" % t, [P, 2 * S], F32))
+            nc.vector.memset(y_sb[t][:, S:], 0.0)
+            size.append(tile("size%d" % t, [P, 2 * S], F32))
+            nc.gpsimd.memset(size[t][:, S:], 0.0)
+        warm = tile("warm", [P, 1], F32)
+        nc.scalar.activation(out=warm[:], in_=half_c[:], func=ACT.Abs_reciprocal_sqrt, bias=half_c[:], scale=1.0)
 
         hz_bytes = tile("hz_bytes", [P, S], U8)
         nc.vector.tensor_copy(hz_bytes[:], xs[:].indirect(hz_t[:]))
@@ -79,87 +88,30 @@ def tile_picked_twhnormbpaget_none_p_kernel(
             nc.scalar.dma_start(hz_plane[r:P:32, :].bitcast(I32), hz_bytes[16 + r : P : 32, :].bitcast(I32))
         tok_plane = tile("tok_plane", [P, S], U8)
         nc.vector.tensor_copy(tok_plane[:], xs[:].indirect(offs_t[:]))
-        tok_words = tile("tok_words", [P, S], U32)
-        nc.vector.tensor_copy(tok_words[:], xw[:].indirect(offs_t[:]))
         hz_words = tile("hz_words", [P, S], U32)
         nc.vector.tensor_copy(hz_words[:], xw[:].indirect(hz_t[:]))
+        tok_words = tile("tok_words", [P, S], U32)
+        nc.vector.tensor_copy(tok_words[:], xw[:].indirect(offs_t[:]))
 
-        def dealt_views(grouped, raw, ts):
-            dst = grouped[:].rearrange("p (t m j) -> p m j t", t=PACK, j=PACK)[:, :, :, ts]
-            src = raw[:].rearrange("p j (m t) -> p m j t", t=PACK)[:, :, :, ts]
-            return dst, src
+        def quantize(name, grouped):
+            codes = tile(name + "_codes", [P, 512], U32)
+            plane = tile(name + "_plane", [P, 512], U8)
+            nc.vector.quantize_mx(out=codes[:].bitcast(FP8X4), scales=plane[:], in_=grouped[:])
+            return codes, plane
 
-        def quantize(codes, plane, grouped, cols):
-            nc.vector.quantize_mx(
-                out=codes[:, cols].bitcast(FP8X4),
-                scales=plane[:, cols],
-                in_=grouped[:, PACK * cols.start : PACK * cols.stop],
-            )
-
-        def product(acc, w_codes, w_plane, t, words, plane):
+        def product(bank, weights, t, words, plane):
+            acc = psum.tile([P, S], F32, name=bank)
             cols = slice(t * P, (t + 1) * P)
             nc.tensor.matmul_mx(
-                out=acc,
-                lhsT=w_codes[:, cols].bitcast(FP8X4),
-                lhsT_scale=w_plane[:, cols],
-                rhs=words.bitcast(FP8X4),
-                rhs_scale=plane,
+                out=acc[:],
+                lhsT=weights[0][:, cols].bitcast(FP8X4),
+                lhsT_scale=weights[1][:, cols],
+                rhs=words[:].bitcast(FP8X4),
+                rhs_scale=plane[:],
                 start=True,
                 stop=True,
             )
-
-        w1_bf = tile("w1_bf", [P, PACK * H], BF16)
-        w1_codes = tile("w1_codes", [P, H], U32)
-        w1_plane = tile("w1_plane", [P, H], U8)
-        dst, src = dealt_views(w1_bf, w1_raw, slice(0, 2))
-        nc.scalar.activation(out=dst, in_=src, func=ACT.Copy)
-        dst, src = dealt_views(w1_bf, w1_raw, slice(2, 4))
-        nc.vector.tensor_copy(dst, src)
-        quantize(w1_codes, w1_plane, w1_bf, halves[1])
-        quantize(w1_codes, w1_plane, w1_bf, halves[0])
-        order = [2, 3, 0, 1]
-        y_ps, y_sb = {}, {}
-        for t in order:
-            y_ps[t] = psum.tile([P, S], F32, name="bank_y%d" % t)
-            product(y_ps[t][:], w1_codes, w1_plane, t, tok_words[:], tok_plane[:])
-        for t in order:
-            y_sb[t] = tile("y_sb%d" % t, [P, S], F32)
-            nc.scalar.copy(y_sb[t][:], y_ps[t][:])
-
-        w2_bf = tile("w2_bf", [P, PACK * H], BF16)
-        w2_codes = tile("w2_codes", [P, H], U32)
-        w2_plane = tile("w2_plane", [P, H], U8)
-        dst, src = dealt_views(w2_bf, w2_raw, slice(0, 4))
-        nc.vector.tensor_copy(dst, src)
-        quantize(w2_codes, w2_plane, w2_bf, slice(0, H))
-        size = {}
-        for t in order:
-            d_ps = psum.tile([P, S], F32, name="bank_d%d" % t)
-            product(d_ps[:], w2_codes, w2_plane, t, hz_words[:], hz_plane[:])
-            size[t] = tile("size%d" % t, [P, S], F32)
-            nc.scalar.activation(out=size[t][:], in_=d_ps[:], func=ACT.Abs)
-
-        y_far = tile("y_far", [P, PACK, S], F32)
-        size_far = tile("size_far", [P, PACK, S], F32)
-        num = tile("num", [P, PACK, S], F32)
-        den = tile("den", [P, PACK, S], F32)
-        root = tile("root", [P, PACK, S], F32)
-        part = tile("part", [P, PACK, S], F32)
-        w3_bf = tile("w3_bf", [P, PACK * N], BF16)
-        w3_codes = tile("w3_codes", [P, N], U32)
-        w3_plane = tile("w3_plane", [P, N], U8)
-        z_bf = tile("z_bf", [P, PACK * S], BF16)
-        z_codes = tile("z_codes", [P, S], U32)
-        z_plane = tile("z_plane", [P, S], U8)
-        quads = [slice(0, HALF // 4), slice(HALF // 4, S // 4)]
-        old, gate, gap, step, new, h_ps = {}, {}, {}, {}, {}, {}
-        for u in range(4):
-            old[u] = tile("old%d" % u, [P, S], F32)
-            gate[u] = tile("gate%d" % u, [P, S], F32)
-            gap[u] = tile("gap%d" % u, [P, S], F32)
-            step[u] = tile("step%d" % u, [P, S], F32)
-        for u in range(3):
-            new[u] = tile("new%d" % u, [P, S], F32)
+            return acc
 
         def fetch(on_scalar, dst, window):
             if on_scalar:
@@ -167,134 +119,124 @@ def tile_picked_twhnormbpaget_none_p_kernel(
             else:
                 nc.vector.tensor_copy(dst, window)
 
-        def fetch_y(on_scalar, t, a):
-            fetch(on_scalar, y_far[:, t, halves[a]], y_sb[t][:].indirect(n1_t[:, list_halves[a]]))
-
-        def fetch_size(t, a):
-            fetch(True, size_far[:, t, halves[a]], size[t][:].indirect(n2_t[:, list_halves[a]]))
-
-        def make_num(t, a):
-            nc.vector.tensor_tensor(num[:, t, halves[a]], y_ps[t][:, halves[a]], y_far[:, t, halves[a]], ALU.subtract)
-
-        def make_den(t, a):
-            nc.vector.tensor_tensor(den[:, t, halves[a]], size[t][:, halves[a]], size_far[:, t, halves[a]], ALU.add)
-
-        def make_root(a):
+        w2_bf = tile("w2_bf", [P, PACK * H], BF16)
+        w2_dealt = w2_bf[:].rearrange("p (t m j) -> p m j t", t=PACK, j=PACK)
+        for a in range(2):
             nc.scalar.activation(
-                out=root[:, :, halves[a]], in_=den[:, :, halves[a]], func=ACT.Abs_reciprocal_sqrt, bias=half_c[:], scale=1.0
+                out=w2_dealt[:, 64 * a : 64 * (a + 1)],
+                in_=w2_raw[a][:].rearrange("p j (m t) -> p m j t", t=PACK),
+                func=ACT.Copy,
             )
+        w2_mx = quantize("w2", w2_bf)
+        for t in range(PACK):
+            d_ps = product("bank_d%d" % t, w2_mx, t, hz_words, hz_plane)
+            nc.scalar.activation(out=size[t][:, :S], in_=d_ps[:], func=ACT.Abs)
 
-        def make_part(t, a):
+        w1_bf = tile("w1_bf", [P, PACK * H], BF16)
+        nc.vector.tensor_copy(
+            w1_bf[:].rearrange("p (t m j) -> p m j t", t=PACK, j=PACK),
+            w1_raw[:].rearrange("p j (m t) -> p m j t", t=PACK),
+        )
+        w1_mx = quantize("w1", w1_bf)
+        y_ps = []
+        for t in range(PACK):
+            y_ps.append(product("bank_y%d" % t, w1_mx, t, tok_words, tok_plane))
+            nc.scalar.copy(y_sb[t][:, :S], y_ps[t][:])
+
+        y_far = tile("y_far", [P, PACK, S], F32)
+        size_far = tile("size_far", [P, PACK, S], F32, "w1_bf")
+        num = tile("num", [P, PACK, S], F32)
+        den = [tile("den%d" % t, [P, S], F32) for t in range(PACK)]
+        root = tile("root", [P, PACK, S], F32)
+        part = tile("part", [P, PACK, S], F32)
+        w3_bf = tile("w3_bf", [P, PACK * N], BF16)
+        z_bf = tile("z_bf", [P, PACK * S], BF16)
+        w3_dst = w3_bf[:].rearrange("p (c i j) -> p c j i", i=4, j=PACK)
+        w3_src = w3_raw[:].rearrange("p j (c i) -> p c j i", i=4)
+
+        for t in range(PACK):
+            fetch(False, size_far[:, t, :], size[t][:].indirect(n2_t[:]))
+        for t in range(PACK):
+            nc.gpsimd.tensor_tensor(den[t][:], size[t][:, :S], size_far[:, t, :], ALU.add)
+        nc.vector.tensor_copy(w3_dst, w3_src)
+
+        for t in range(PACK):
+            fetch(t >= 0, y_far[:, t, :], y_sb[t][:].indirect(n1_t[:]))
+        w3_mx = quantize("w3", w3_bf)
+        for t in range(PACK):
+            nc.vector.tensor_tensor(num[:, t, :], y_ps[t][:], y_far[:, t, :], ALU.subtract)
+        for t in range(PACK):
+            nc.scalar.activation(
+                out=root[:, t, :], in_=den[t][:], func=ACT.Abs_reciprocal_sqrt, bias=half_c[:], scale=1.0
+            )
+        for t in range(PACK):
             nc.vector.scalar_tensor_tensor(
-                part[:, t, halves[a]], num[:, t, halves[a]], gn_t[:, t : t + 1], root[:, t, halves[a]], ALU.mult, ALU.mult
+                part[:, t, :], num[:, t, :], gn_t[:, t : t + 1], root[:, t, :], ALU.mult, ALU.mult
             )
+        old_first = tile("old_first", [P, 3, S], F32, "den%d" % (PACK - 1))
+        old = [old_first[:, u, :] for u in range(3)]
+        for u in range(3):
+            fetch(True, old[u], page[u][:].indirect(n3_t[:]))
+        nc.vector.tensor_tensor(
+            z_bf[:].rearrange("p (c i t) -> p c t i", i=4, t=PACK),
+            part[:].rearrange("p t (c i) -> p c t i", i=4),
+            root[:].rearrange("p t (c i) -> p c t i", i=4),
+            ALU.mult,
+        )
+        z_codes, z_plane = quantize("z", z_bf)
+        h_ps = [product("bank_d%d" % u, w3_mx, u, z_codes, z_plane) for u in range(4)]
+        old_last = tile("old_last", [P, 1, S], F32, "z_bf")
+        for u in range(3, 4):
+            old.append(old_last[:, u - 3, :])
+            fetch(False, old[u], page[u][:].indirect(n3_t[:]))
 
-        def make_z(a):
-            nc.vector.tensor_tensor(
-                z_bf[:].rearrange("p (c i t) -> p c t i", i=4, t=PACK)[:, quads[a]],
-                part[:].rearrange("p t (c i) -> p c t i", i=4)[:, quads[a]],
-                root[:].rearrange("p t (c i) -> p c t i", i=4)[:, quads[a]],
-                ALU.mult,
-            )
+        gate = [tile("gate%d" % u, [P, S], F32) for u in range(4)]
+        gap = [tile("gap%d" % u, [P, S], F32) for u in range(4)]
+        step = [tile("step%d" % u, [P, S], F32) for u in range(4)]
+        new = [tile("new%d" % u, [P, S], F32) for u in range(3)]
 
-        def make_h(a):
-            quantize(z_codes, z_plane, z_bf, halves[a])
-            for u in range(4):
-                bank = psum.tile([P, S], F32, name=("bank_d%d", "bank_y%d")[a] % u)
-                h_ps[u, a] = bank[:, 0:HALF]
-                product(h_ps[u, a], w3_codes, w3_plane, u, z_codes[:, halves[a]], z_plane[:, halves[a]])
+        def make_gap(u):
+            nc.vector.tensor_tensor(gap[u][:], h_ps[u][:], old[u], ALU.subtract)
 
-        def fetch_old(on_scalar, u):
-            fetch(on_scalar, old[u][:], page[u][:].indirect(n3_t[:]))
-
-        def make_gate(u, a):
-            nc.scalar.activation(out=gate[u][:, halves[a]], in_=h_ps[u, a], func=ACT.Sigmoid)
-
-        def make_gap(u, a):
-            nc.vector.tensor_tensor(gap[u][:, halves[a]], h_ps[u, a], old[u][:, halves[a]], ALU.subtract)
-
-        def make_step(u):
-            nc.vector.tensor_tensor(step[u][:], gap[u][:], gate[u][:], ALU.mult)
+        def make_step(u, cols):
+            nc.vector.tensor_tensor(step[u][:, cols], gap[u][:, cols], gate[u][:, cols], ALU.mult)
 
         def make_new(u, cols):
             nc.vector.tensor_tensor(new[u][:, cols], step[u][:, cols], old[u][:, cols], ALU.add)
 
-        def put_scalar(u, a):
-            nc.scalar.activation(
-                out=page[u][:].indirect(n3_t[:, list_halves[a]]), in_=new[u][:, halves[a]], func=ACT.Copy
-            )
+        def slots(u, cols):
+            return page[u][:].indirect(n3_t[:, cols.start // 16 : cols.stop // 16])
 
-        def store(u):
-            nc.sync.dma_start(out[u * P : (u + 1) * P, :], page[u][:])
+        def put_scalar(u, cols):
+            nc.scalar.activation(out=slots(u, cols), in_=new[u][:, cols], func=ACT.Copy)
 
-        for t in order:
-            fetch_y(False, t, 0)
-        for a in range(2):
-            for t in order:
-                fetch_size(t, a)
-        for t in order:
-            make_num(t, 0)
-        nc.vector.tensor_copy(
-            w3_bf[:].rearrange("p (c i j) -> p c j i", i=4, j=PACK),
-            w3_raw[:].rearrange("p j (c i) -> p c j i", i=4),
-        )
-        for t in order:
-            make_den(t, 0)
-        quantize(w3_codes, w3_plane, w3_bf, slice(0, N))
-        for t in order[:2]:
-            fetch_y(True, t, 1)
-        for t in order:
-            make_den(t, 1)
-        for t in order[2:]:
-            fetch_y(False, t, 1)
-        make_root(0)
-        make_root(1)
-        for t in order:
-            make_num(t, 1)
-        for t in order:
-            make_part(t, 0)
-        fetch_old(True, 0)
-        make_part(order[0], 1)
-        make_z(0)
-        make_part(order[1], 1)
-        make_h(0)
-        for t in order[2:]:
-            make_part(t, 1)
-        make_gate(0, 0)
-        fetch_old(True, 1)
-        make_gap(0, 0)
-        make_z(1)
-        make_gap(1, 0)
-        make_h(1)
-        for u in range(1, 4):
-            make_gate(u, 0)
+        def put_vector(u, cols):
+            nc.vector.tensor_tensor(slots(u, cols), step[u][:, cols], old[u][:, cols], ALU.add)
+
+        def store(queue, u):
+            queue.dma_start(out[u * P : (u + 1) * P, :], page[u][:])
+
+        for u in range(4):
+            nc.scalar.activation(out=gate[u][:], in_=h_ps[u][:], func=ACT.Sigmoid)
+        make_gap(0)
+        for cols in halves:
+            make_step(0, cols)
+        for cols in halves:
+            make_new(0, cols)
+        make_gap(1)
+        make_gap(2)
+        make_step(1, whole)
+        make_step(2, whole)
+        make_new(1, whole)
+        make_gap(3)
+        make_new(2, slice(0, SCALAR_SHARE))
+        make_step(3, whole)
         for u in range(2):
-            make_gate(u, 1)
-        fetch_old(False, 2)
-        make_gap(0, 1)
-        make_gap(1, 1)
-        make_step(0)
-        fetch_old(True, 3)
-        for u in range(2, 4):
-            make_gate(u, 1)
-        make_step(1)
-        make_new(0, slice(0, S))
-        make_gap(2, 0)
-        make_new(1, slice(0, S))
-        make_gap(2, 1)
-        for u in range(2):
-            put_scalar(u, 0)
-            put_scalar(u, 1)
-            store(u)
-        make_gap(3, 0)
-        make_step(2)
-        make_gap(3, 1)
-        make_new(2, halves[0])
-        make_step(3)
-        nc.vector.tensor_tensor(
-            page[2][:].indirect(n3_t[:, list_halves[1]]), step[2][:, halves[1]], old[2][:, halves[1]], ALU.add
-        )
-        put_scalar(2, 0)
-        nc.vector.tensor_tensor(page[3][:].indirect(n3_t[:]), step[3][:], old[3][:], ALU.add)
-        store(3)
-        store(2)
+            for cols in halves:
+                put_scalar(u, cols)
+            store(nc.sync, u)
+        put_vector(2, slice(SCALAR_SHARE, S))
+        put_vector(3, whole)
+        store(nc.sync, 3)
+        put_scalar(2, slice(0, SCALAR_SHARE))
+        store(nc.scalar, 2)

@@ -57,14 +57,14 @@ def tile_picked_twhnormbpaget_none_p_kernel(
         offs_t = load_list("offs_t", offs)
         xw = tile("xw", [P, T], U32)
         nc.sync.dma_start(xw[:].bitcast(I32), x_words[0].rearrange("p n t -> p (n t)").bitcast(I32))
-        w2_raw = [load_weight("w2_raw%d" % a, w2, halves[a]) for a in range(2)]
-        w1_raw = load_weight("w1_raw", w1, whole)
+        w1_raw = [load_weight("w1_raw%d" % a, w1, halves[a]) for a in range(2)]
+        w2_raw = load_weight("w2_raw", w2, whole)
+        w3_raw = load_weight("w3_raw", w3, whole)
         n2_t = load_list("n2_t", n2)
         n1_t = load_list("n1_t", n1)
         gn_t = tile("gn_t", [P, PACK], F32)
         nc.sync.dma_start(gn_t[:], gn.rearrange("(p t) o -> p (t o)", t=PACK))
         n3_t = load_list("n3_t", n3)
-        w3_raw = load_weight("w3_raw", w3, whole)
         page = []
         for u in range(4):
             page.append(tile("page%d" % u, [P, U], F32))
@@ -76,7 +76,7 @@ def tile_picked_twhnormbpaget_none_p_kernel(
             y_sb.append(tile("y_sb%d" % t, [P, 2 * S], F32))
             nc.vector.memset(y_sb[t][:, S:], 0.0)
             size.append(tile("size%d" % t, [P, 2 * S], F32))
-            nc.gpsimd.memset(size[t][:, S:], 0.0)
+            nc.scalar.copy(size[t][:, S:], y_sb[t][:, S:])
         warm = tile("warm", [P, 1], F32)
         nc.scalar.activation(out=warm[:], in_=half_c[:], func=ACT.Abs_reciprocal_sqrt, bias=half_c[:], scale=1.0)
 
@@ -88,10 +88,10 @@ def tile_picked_twhnormbpaget_none_p_kernel(
             nc.scalar.dma_start(hz_plane[r:P:32, :].bitcast(I32), hz_bytes[16 + r : P : 32, :].bitcast(I32))
         tok_plane = tile("tok_plane", [P, S], U8)
         nc.vector.tensor_copy(tok_plane[:], xs[:].indirect(offs_t[:]))
-        hz_words = tile("hz_words", [P, S], U32)
-        nc.vector.tensor_copy(hz_words[:], xw[:].indirect(hz_t[:]))
         tok_words = tile("tok_words", [P, S], U32)
         nc.vector.tensor_copy(tok_words[:], xw[:].indirect(offs_t[:]))
+        hz_words = tile("hz_words", [P, S], U32)
+        nc.vector.tensor_copy(hz_words[:], xw[:].indirect(hz_t[:]))
 
         def quantize(name, grouped):
             codes = tile(name + "_codes", [P, 512], U32)
@@ -119,32 +119,31 @@ def tile_picked_twhnormbpaget_none_p_kernel(
             else:
                 nc.vector.tensor_copy(dst, window)
 
-        w2_bf = tile("w2_bf", [P, PACK * H], BF16)
-        w2_dealt = w2_bf[:].rearrange("p (t m j) -> p m j t", t=PACK, j=PACK)
+        w1_bf = tile("w1_bf", [P, PACK * H], BF16)
+        w1_dealt = w1_bf[:].rearrange("p (t m j) -> p m j t", t=PACK, j=PACK)
         for a in range(2):
             nc.scalar.activation(
-                out=w2_dealt[:, 64 * a : 64 * (a + 1)],
-                in_=w2_raw[a][:].rearrange("p j (m t) -> p m j t", t=PACK),
+                out=w1_dealt[:, 64 * a : 64 * (a + 1)],
+                in_=w1_raw[a][:].rearrange("p j (m t) -> p m j t", t=PACK),
                 func=ACT.Copy,
             )
-        w2_mx = quantize("w2", w2_bf)
-        for t in range(PACK):
-            d_ps = product("bank_d%d" % t, w2_mx, t, hz_words, hz_plane)
-            nc.scalar.activation(out=size[t][:, :S], in_=d_ps[:], func=ACT.Abs)
-
-        w1_bf = tile("w1_bf", [P, PACK * H], BF16)
-        nc.vector.tensor_copy(
-            w1_bf[:].rearrange("p (t m j) -> p m j t", t=PACK, j=PACK),
-            w1_raw[:].rearrange("p j (m t) -> p m j t", t=PACK),
-        )
         w1_mx = quantize("w1", w1_bf)
         y_ps = []
         for t in range(PACK):
             y_ps.append(product("bank_y%d" % t, w1_mx, t, tok_words, tok_plane))
             nc.scalar.copy(y_sb[t][:, :S], y_ps[t][:])
 
-        y_far = tile("y_far", [P, PACK, S], F32)
-        size_far = tile("size_far", [P, PACK, S], F32, "w1_bf")
+        w2_bf = tile("w2_bf", [P, PACK * H], BF16)
+        nc.vector.tensor_copy(
+            w2_bf[:].rearrange("p (t m j) -> p m j t", t=PACK, j=PACK),
+            w2_raw[:].rearrange("p j (m t) -> p m j t", t=PACK),
+        )
+        w2_mx = quantize("w2", w2_bf)
+        for t in range(PACK):
+            d_ps = product("bank_d%d" % t, w2_mx, t, hz_words, hz_plane)
+            nc.scalar.activation(out=size[t][:, :S], in_=d_ps[:], func=ACT.Abs)
+
+        y_far = tile("y_far", [P, PACK, S], F32, "w2_codes")
         num = tile("num", [P, PACK, S], F32)
         den = [tile("den%d" % t, [P, S], F32) for t in range(PACK)]
         root = tile("root", [P, PACK, S], F32)
@@ -153,16 +152,17 @@ def tile_picked_twhnormbpaget_none_p_kernel(
         z_bf = tile("z_bf", [P, PACK * S], BF16)
         w3_dst = w3_bf[:].rearrange("p (c i j) -> p c j i", i=4, j=PACK)
         w3_src = w3_raw[:].rearrange("p j (c i) -> p c j i", i=4)
+        nc.vector.tensor_copy(w3_dst, w3_src)
+        w3_mx = quantize("w3", w3_bf)
+        size_far = tile("size_far", [P, PACK, S], F32, "w3_bf")
 
         for t in range(PACK):
             fetch(False, size_far[:, t, :], size[t][:].indirect(n2_t[:]))
         for t in range(PACK):
             nc.gpsimd.tensor_tensor(den[t][:], size[t][:, :S], size_far[:, t, :], ALU.add)
-        nc.vector.tensor_copy(w3_dst, w3_src)
 
         for t in range(PACK):
-            fetch(t >= 0, y_far[:, t, :], y_sb[t][:].indirect(n1_t[:]))
-        w3_mx = quantize("w3", w3_bf)
+            fetch(True, y_far[:, t, :], y_sb[t][:].indirect(n1_t[:]))
         for t in range(PACK):
             nc.vector.tensor_tensor(num[:, t, :], y_ps[t][:], y_far[:, t, :], ALU.subtract)
         for t in range(PACK):
@@ -216,14 +216,14 @@ def tile_picked_twhnormbpaget_none_p_kernel(
         def store(queue, u):
             queue.dma_start(out[u * P : (u + 1) * P, :], page[u][:])
 
-        for u in range(4):
-            nc.scalar.activation(out=gate[u][:], in_=h_ps[u][:], func=ACT.Sigmoid)
         make_gap(0)
+        for u in (1, 0, 2, 3):
+            nc.scalar.activation(out=gate[u][:], in_=h_ps[u][:], func=ACT.Sigmoid)
+        make_gap(1)
         for cols in halves:
             make_step(0, cols)
         for cols in halves:
             make_new(0, cols)
-        make_gap(1)
         make_gap(2)
         make_step(1, whole)
         make_step(2, whole)

from contextlib import ExitStack

import concourse.mybir as mybir

K, T, S, H, N, U = 512, 2048, 512, 512, 512, 1024
FLOPS = 2 * S * (2 * K * H + H * N)

F32 = mybir.dt.float32
BF16 = mybir.dt.bfloat16
I32 = mybir.dt.int32
U32 = mybir.dt.uint32
U16 = mybir.dt.uint16
U8 = mybir.dt.uint8
FP8X4 = mybir.dt.float8_e4m3fn_x4
ALU = mybir.AluOpType
ACT = mybir.ActivationFunctionType

P = 128
PACK = 4
HALF = S // 2
LIST_COLS = S // 16
SCALAR_SHARE = 320


def tile_picked_twhnormbpaget_none_p_kernel(
    tc, x_words, x_scales, w1, w2, gn, w3, mem, offs, hz, n1, n2, n3, out
):
    nc = tc.nc
    whole = slice(0, S)
    halves = [slice(0, HALF), slice(HALF, S)]

    with ExitStack() as ctx:
        sb = ctx.enter_context(tc.tile_pool(name="sb", bufs=1))
        psum = ctx.enter_context(tc.psum_pool(name="psum", bufs=1))

        def tile(name, shape, dtype, tag=None):
            return sb.tile(shape, dtype, name=name, tag=tag or name, align_bytes=64)

        def load_list(name, src):
            dst = tile(name, [P, LIST_COLS], U16)
            nc.sync.dma_start(dst[:], src)
            return dst

        def load_weight(name, src, cols):
            dst = tile(name, [P, PACK, cols.stop - cols.start], F32)
            nc.sync.dma_start(dst[:], src.rearrange("(p j) c -> p j c", j=PACK)[:, :, cols])
            return dst

        xs = tile("xs", [P, T], U8)
        rows = x_scales[0].bitcast(I32)
        for q in range(4):
            nc.sync.dma_start(
                xs[32 * q : 32 * (q + 1), :].bitcast(I32),
                rows[4 * q : 4 * (q + 1), :].unsqueeze(0).broadcast_to([8, 4, T // 4]),
            )
        hz_t = load_list("hz_t", hz)
        offs_t = load_list("offs_t", offs)
        xw = tile("xw", [P, T], U32)
        nc.sync.dma_start(xw[:].bitcast(I32), x_words[0].rearrange("p n t -> p (n t)").bitcast(I32))
        w1_raw = [load_weight("w1_raw%d" % a, w1, halves[a]) for a in range(2)]
        w2_raw = load_weight("w2_raw", w2, whole)
        w3_raw = load_weight("w3_raw", w3, whole)
        n2_t = load_list("n2_t", n2)
        n1_t = load_list("n1_t", n1)
        gn_t = tile("gn_t", [P, PACK], F32)
        nc.sync.dma_start(gn_t[:], gn.rearrange("(p t) o -> p (t o)", t=PACK))
        n3_t = load_list("n3_t", n3)
        page = []
        for u in range(4):
            page.append(tile("page%d" % u, [P, U], F32))
            nc.sync.dma_start(page[u][:], mem[u * P : (u + 1) * P, :])
        half_c = tile("half_c", [P, 1], F32)
        nc.gpsimd.memset(half_c[:], 0.5)
        y_sb, size = [], []
        for t in range(PACK):
            y_sb.append(tile("y_sb%d" % t, [P, 2 * S], F32))
            nc.vector.memset(y_sb[t][:, S:], 0.0)
            size.append(tile("size%d" % t, [P, 2 * S], F32))
            nc.scalar.copy(size[t][:, S:], y_sb[t][:, S:])
        warm = tile("warm", [P, 1], F32)
        nc.scalar.activation(out=warm[:], in_=half_c[:], func=ACT.Abs_reciprocal_sqrt, bias=half_c[:], scale=1.0)

        hz_bytes = tile("hz_bytes", [P, S], U8)
        nc.vector.tensor_copy(hz_bytes[:], xs[:].indirect(hz_t[:]))
        hz_plane = tile("hz_plane", [P, S], U8)
        nc.vector.tensor_copy(hz_plane[:].bitcast(I32), hz_bytes[:].bitcast(I32))
        for r in range(2, 4):
            nc.scalar.dma_start(hz_plane[r:P:32, :].bitcast(I32), hz_bytes[16 + r : P : 32, :].bitcast(I32))
        tok_plane = tile("tok_plane", [P, S], U8)
        nc.vector.tensor_copy(tok_plane[:], xs[:].indirect(offs_t[:]))
        tok_words = tile("tok_words", [P, S], U32)
        nc.vector.tensor_copy(tok_words[:], xw[:].indirect(offs_t[:]))
        hz_words = tile("hz_words", [P, S], U32)
        nc.vector.tensor_copy(hz_words[:], xw[:].indirect(hz_t[:]))

        def quantize(name, grouped):
            codes = tile(name + "_codes", [P, 512], U32)
            plane = tile(name + "_plane", [P, 512], U8)
            nc.vector.quantize_mx(out=codes[:].bitcast(FP8X4), scales=plane[:], in_=grouped[:])
            return codes, plane

        def product(bank, weights, t, words, plane):
            acc = psum.tile([P, S], F32, name=bank)
            cols = slice(t * P, (t + 1) * P)
            nc.tensor.matmul_mx(
                out=acc[:],
                lhsT=weights[0][:, cols].bitcast(FP8X4),
                lhsT_scale=weights[1][:, cols],
                rhs=words[:].bitcast(FP8X4),
                rhs_scale=plane[:],
                start=True,
                stop=True,
            )
            return acc

        def fetch(on_scalar, dst, window):
            if on_scalar:
                nc.scalar.activation(out=dst, in_=window, func=ACT.Copy)
            else:
                nc.vector.tensor_copy(dst, window)

        w1_bf = tile("w1_bf", [P, PACK * H], BF16)
        w1_dealt = w1_bf[:].rearrange("p (t m j) -> p m j t", t=PACK, j=PACK)
        for a in range(2):
            nc.scalar.activation(
                out=w1_dealt[:, 64 * a : 64 * (a + 1)],
                in_=w1_raw[a][:].rearrange("p j (m t) -> p m j t", t=PACK),
                func=ACT.Copy,
            )
        w1_mx = quantize("w1", w1_bf)
        y_ps = []
        for t in range(PACK):
            y_ps.append(product("bank_y%d" % t, w1_mx, t, tok_words, tok_plane))
            nc.scalar.copy(y_sb[t][:, :S], y_ps[t][:])

        w2_bf = tile("w2_bf", [P, PACK * H], BF16)
        nc.vector.tensor_copy(
            w2_bf[:].rearrange("p (t m j) -> p m j t", t=PACK, j=PACK),
            w2_raw[:].rearrange("p j (m t) -> p m j t", t=PACK),
        )
        w2_mx = quantize("w2", w2_bf)
        for t in range(PACK):
            d_ps = product("bank_d%d" % t, w2_mx, t, hz_words, hz_plane)
            nc.scalar.activation(out=size[t][:, :S], in_=d_ps[:], func=ACT.Abs)

        y_far = tile("y_far", [P, PACK, S], F32, "w2_codes")
        num = tile("num", [P, PACK, S], F32)
        den = [tile("den%d" % t, [P, S], F32) for t in range(PACK)]
        root = tile("root", [P, PACK, S], F32)
        part = tile("part", [P, PACK, S], F32)
        w3_bf = tile("w3_bf", [P, PACK * N], BF16)
        z_bf = tile("z_bf", [P, PACK * S], BF16)
        w3_dst = w3_bf[:].rearrange("p (c i j) -> p c j i", i=4, j=PACK)
        w3_src = w3_raw[:].rearrange("p j (c i) -> p c j i", i=4)
        nc.vector.tensor_copy(w3_dst, w3_src)
        w3_mx = quantize("w3", w3_bf)
        size_far = tile("size_far", [P, PACK, S], F32, "w3_bf")

        for t in range(PACK):
            fetch(False, size_far[:, t, :], size[t][:].indirect(n2_t[:]))
        for t in range(PACK):
            nc.gpsimd.tensor_tensor(den[t][:], size[t][:, :S], size_far[:, t, :], ALU.add)

        for t in range(PACK):
            fetch(True, y_far[:, t, :], y_sb[t][:].indirect(n1_t[:]))
        for t in range(PACK):
            nc.vector.tensor_tensor(num[:, t, :], y_ps[t][:], y_far[:, t, :], ALU.subtract)
        for t in range(PACK):
            nc.scalar.activation(
                out=root[:, t, :], in_=den[t][:], func=ACT.Abs_reciprocal_sqrt, bias=half_c[:], scale=1.0
            )
        for t in range(PACK):
            nc.vector.scalar_tensor_tensor(
                part[:, t, :], num[:, t, :], gn_t[:, t : t + 1], root[:, t, :], ALU.mult, ALU.mult
            )
        old_first = tile("old_first", [P, 3, S], F32, "den%d" % (PACK - 1))
        old = [old_first[:, u, :] for u in range(3)]
        for u in range(3):
            fetch(True, old[u], page[u][:].indirect(n3_t[:]))
        nc.vector.tensor_tensor(
            z_bf[:].rearrange("p (c i t) -> p c t i", i=4, t=PACK),
            part[:].rearrange("p t (c i) -> p c t i", i=4),
            root[:].rearrange("p t (c i) -> p c t i", i=4),
            ALU.mult,
        )
        z_codes, z_plane = quantize("z", z_bf)
        h_ps = [product("bank_d%d" % u, w3_mx, u, z_codes, z_plane) for u in range(4)]
        old_last = tile("old_last", [P, 1, S], F32, "z_bf")
        for u in range(3, 4):
            old.append(old_last[:, u - 3, :])
            fetch(False, old[u], page[u][:].indirect(n3_t[:]))

        gate = [tile("gate%d" % u, [P, S], F32) for u in range(4)]
        gap = [tile("gap%d" % u, [P, S], F32) for u in range(4)]
        step = [tile("step%d" % u, [P, S], F32) for u in range(4)]
        new = [tile("new%d" % u, [P, S], F32) for u in range(3)]

        def make_gap(u):
            nc.vector.tensor_tensor(gap[u][:], h_ps[u][:], old[u], ALU.subtract)

        def make_step(u, cols):
            nc.vector.tensor_tensor(step[u][:, cols], gap[u][:, cols], gate[u][:, cols], ALU.mult)

        def make_new(u, cols):
            nc.vector.tensor_tensor(new[u][:, cols], step[u][:, cols], old[u][:, cols], ALU.add)

        def slots(u, cols):
            return page[u][:].indirect(n3_t[:, cols.start // 16 : cols.stop // 16])

        def put_scalar(u, cols):
            nc.scalar.activation(out=slots(u, cols), in_=new[u][:, cols], func=ACT.Copy)

        def put_vector(u, cols):
            nc.vector.tensor_tensor(slots(u, cols), step[u][:, cols], old[u][:, cols], ALU.add)

        def store(queue, u):
            queue.dma_start(out[u * P : (u + 1) * P, :], page[u][:])

        make_gap(0)
        for u in (1, 0, 2, 3):
            nc.scalar.activation(out=gate[u][:], in_=h_ps[u][:], func=ACT.Sigmoid)
        make_gap(1)
        for cols in halves:
            make_step(0, cols)
        for cols in halves:
            make_new(0, cols)
        make_gap(2)
        make_step(1, whole)
        make_step(2, whole)
        make_new(1, whole)
        make_gap(3)
        make_new(2, slice(0, SCALAR_SHARE))
        make_step(3, whole)
        for u in range(2):
            for cols in halves:
                put_scalar(u, cols)
            store(nc.sync, u)
        put_vector(2, slice(SCALAR_SHARE, S))
        put_vector(3, whole)
        store(nc.sync, 3)
        put_scalar(2, slice(0, SCALAR_SHARE))
        store(nc.scalar, 2)
